import numpy as np
import ml_dtypes


def mxq(x, axis, fmt="e4m3"):
    dtype, down = {"e4m3": (ml_dtypes.float8_e4m3fn, 7), "e5m2": (ml_dtypes.float8_e5m2, 14)}[fmt]
    v = np.moveaxis(np.asarray(x, np.float32).astype(ml_dtypes.bfloat16).astype(np.float64), axis, -1)
    blocks = v.reshape(v.shape[:-1] + (-1, 32))
    amax = np.abs(blocks).max(-1, keepdims=True)
    byte = np.maximum(np.where(amax > 0, np.frexp(amax)[1] - 1 + 127, 0) - down, 1)
    scale = np.exp2(byte - 127.0)
    codes = (blocks / scale).astype(np.float32).astype(dtype).astype(np.float64)
    return np.moveaxis((codes * scale).reshape(v.shape), -1, axis)


WIDE = False


def mx_kscale(k):
    if not WIDE:
        return np.ones(k)
    levels = np.array([10, -10, 5, -5, 0])
    if k % 512:
        return np.exp2(np.random.permutation(np.resize(levels, k // 32))).repeat(32)
    a = np.empty((k // 512, 16))
    for p in range(k // 512):
        a[p, :8] = np.random.permutation(np.resize(levels, 8))
        for g in range(8):
            far = levels[np.abs(levels - a[p, g]) >= 10]
            a[p, g + 8] = far[np.random.randint(len(far))]
    return np.exp2(a.ravel()).repeat(32)


def f64(x):
    return np.asarray(x).astype(np.float64)


def striped(idx):
    return np.tile(np.asarray(idx).reshape(-1, 16).T, (8, 1)).astype(np.uint16)


def unstriped(offs):
    return offs[:16].T.reshape(-1).astype(np.int64)


E2M1 = np.array([0.0, 0.5, 1.0, 1.5, 2.0, 3.0, 4.0, 6.0, -0.0, -0.5, -1.0, -1.5, -2.0, -3.0, -4.0, -6.0])


def pack_weight(w, fmt):
    k, n = w.shape
    w = f64(np.asarray(w, np.float32).astype(ml_dtypes.bfloat16)).reshape(k // 32, 32, n)
    amax = np.abs(w).max(1)
    if fmt == "e4m3":
        byte = np.frexp(amax)[1] - 1 + 127 - 7
    else:
        mant, ex = np.frexp(amax / 6.0)
        byte = np.where(mant > 0.5, ex, ex - 1) + 127
    byte = np.clip(np.where(amax > 0, byte, 1), 1, 254)
    scaled = (w * np.exp2(127.0 - byte)[:, None, :]).reshape(k, n).astype(np.float32)
    by_word = np.ascontiguousarray(scaled.reshape(k // 512, 128, 4, n).transpose(0, 1, 3, 2))
    if fmt == "e4m3":
        words = by_word.astype(ml_dtypes.float8_e4m3fn).view(np.uint8)
    else:
        c = by_word.astype(ml_dtypes.float4_e2m1fn).view(np.uint8) & 0xF
        words = (c[..., 0::2] | (c[..., 1::2] << 4)).reshape(k // 512, 128, 2 * n)
    return np.ascontiguousarray(words), np.ascontiguousarray(byte.astype(np.uint8).reshape(k // 512, 16, n))


def unpack_weight(words, scales, fmt):
    g, _, n = scales.shape
    words = np.ascontiguousarray(words).reshape(g, 128, n, -1)
    if fmt == "e4m3":
        vals = words.view(ml_dtypes.float8_e4m3fn).astype(np.float64)
    else:
        nib = np.empty((g, 128, n, 4), np.uint8)
        nib[..., 0::2] = words & 0xF
        nib[..., 1::2] = words >> 4
        vals = E2M1[nib]
    vals = vals * np.repeat(np.exp2(scales.astype(np.float64) - 127.0), 8, axis=1)[..., None]
    return vals.transpose(0, 1, 3, 2).reshape(g * 512, n)


def bf(x):
    return np.asarray(x, np.float32).astype(ml_dtypes.bfloat16)


def planes(Y):
    r, m = Y.shape
    b = f64(bf(Y)).reshape(r // 32, 32, m)
    amax = np.abs(b).max(1)
    byte = np.clip(np.where(amax > 0, np.frexp(amax)[1] - 1 + 127 - 7, 1), 1, 254)
    codes = (b * np.exp2(127.0 - byte)[:, None, :]).reshape(r, m).astype(np.float32).astype(ml_dtypes.float8_e4m3fn).view(np.uint8)
    words = codes.reshape(r // 512, 128, 4, m).transpose(0, 1, 3, 2)
    return np.ascontiguousarray(words), np.ascontiguousarray(byte.astype(np.uint8).reshape(r // 512, 16, m))


D, T, I, Q, E = 512, 2048, 512, 256, 512


def setup_inputs():
    n = np.random.standard_normal
    idx = np.random.permutation(T)[:I]
    idx2 = np.random.permutation(T)[:I]
    idx3 = np.random.permutation(T)[:I]
    fd = mx_kscale(D)
    fi = mx_kscale(I)
    ti = np.ones(T)
    ti[idx3] = fi
    keysp = pack_weight(n((D, T)) / fd[:, None], "e2m1")
    return {
        "query": (n((D, Q)) * 0.6 / np.sqrt(D) * fd[:, None]).astype(np.float32),
        "keys_words": keysp[0],
        "keys_scales": keysp[1],
        "size": (np.random.uniform(0.5, 2.0, (1, I)) * fi).astype(np.float32),
        "vals": (n((E, T)) / ti).astype(np.float32),
        "offs": striped(idx),
        "offs2": striped(idx2),
        "offs3": striped(idx3),
    }


def reference(query, keys_words, keys_scales, size, vals, offs, offs2, offs3):
    idx = unstriped(offs)
    idx2 = unstriped(offs2)
    idx3 = unstriped(offs3)
    keysu = unpack_weight(keys_words, keys_scales, "e2m1")
    queryq = mxq(f64(query), 0, "e4m3")
    keysidxg = keysu[:, idx]
    a = queryq.T @ keysidxg
    keysidx2g = keysu[:, idx2]
    b = queryq.T @ keysidx2g
    s = np.log(np.exp(a) + np.exp(b))
    p = np.exp(s - np.max(s, axis=1, keepdims=True))
    w = p * f64(size) / np.sum(p, axis=1, keepdims=True)
    wt = w.T
    vt = f64(vals)[:, idx3].T
    vtq = mxq(vt, 0, "e4m3")
    wtq = mxq(wt, 0, "e4m3")
    o = vtq.T @ wtq
    words, scales = planes(o)
    return o, words, scales

@@ -1,0 +1,197 @@
+from contextlib import ExitStack
+
+import concourse.mybir as mybir
+from concourse.masks import make_identity
+
+D, T, I, Q, E = 512, 2048, 512, 256, 512
+FLOPS = 2 * (2 * D * Q * I + I * E * Q)
+
+F32 = mybir.dt.float32
+BF16 = mybir.dt.bfloat16
+I32 = mybir.dt.int32
+U32 = mybir.dt.uint32
+U16 = mybir.dt.uint16
+U8 = mybir.dt.uint8
+FP8X4 = mybir.dt.float8_e4m3fn_x4
+FP4X4 = mybir.dt.float4_e2m1fn_x4
+ALU = mybir.AluOpType
+ACT = mybir.ActivationFunctionType
+AX = mybir.AxisListType
+
+P = 128
+PACK = 4
+HALVES = Q // P
+
+
+def tile_attend_synonyms_pl_kernel(tc, query, keys_words, keys_scales, size, vals, offs, offs2, offs3, out_0, out_1, out_2):
+    nc = tc.nc
+    with ExitStack() as ctx:
+        lists = ctx.enter_context(tc.tile_pool(name="lists", bufs=1))
+        sb = ctx.enter_context(tc.tile_pool(name="sb", bufs=1))
+        ps = ctx.enter_context(tc.psum_pool(name="ps", bufs=1))
+
+        key_scales = sb.tile([P, T], U8, name="key_scales", align_bytes=64)
+        nc.vector.memset(key_scales[:].bitcast(I32), 0)
+
+        key_lists = [lists.tile([P, I // 16], U16, name=f"key_list{s}") for s in range(2)]
+        val_list = lists.tile([P, I // 16], U16, name="val_list")
+        nc.sync.dma_start(key_lists[0][:], offs)
+        nc.sync.dma_start(key_lists[1][:], offs2)
+        key_words = sb.tile([P, T], U16, name="key_words", align_bytes=64)
+        nc.sync.dma_start(key_words[:].bitcast(I32), keys_words[0].bitcast(I32))
+        for quad in range(4):
+            nc.sync.dma_start(
+                key_scales[32 * quad : 32 * quad + 4, :].bitcast(I32),
+                keys_scales[0, 4 * quad : 4 * quad + 4, :].bitcast(I32),
+            )
+        q_raw = sb.tile([P, PACK, Q], F32, name="q_raw")
+        nc.sync.dma_start(q_raw[:], query.rearrange("(p t) q -> p t q", t=PACK))
+        nc.sync.dma_start(val_list[:], offs3)
+        val_rows = vals.rearrange("(p t) n -> t p n", t=PACK)
+        val_pool = [sb.tile([P, T], F32, name=f"val_pool{t}") for t in range(PACK)]
+        for t in range(PACK):
+            nc.sync.dma_start(val_pool[t][:], val_rows[t])
+        size_cols = sb.tile([P, PACK], F32, name="size_cols")
+        nc.scalar.dma_start(size_cols[:], size[0].rearrange("(p t) -> p t", t=PACK))
+
+        ident = sb.tile([P, P], F32, name="ident")
+        make_identity(nc, ident[:])
+
+        q_bf = sb.tile([P, Q * PACK], BF16, name="q_bf", align_bytes=64)
+        nc.scalar.copy(
+            q_bf[:].rearrange("p (c i t) -> p c t i", i=4, t=PACK),
+            q_raw[:].rearrange("p t (c i) -> p c t i", i=4),
+        )
+        q_codes = sb.tile([P, Q], U32, name="q_codes", align_bytes=64)
+        q_scales = sb.tile([P, Q], U8, name="q_scales", align_bytes=64)
+
+        kw = [sb.tile([P, I], U16, name=f"kw{s}", align_bytes=64) for s in range(2)]
+        ks = [sb.tile([P, I], U8, name=f"ks{s}", align_bytes=64) for s in range(2)]
+        nc.vector.tensor_copy(kw[0][:], key_words[:].indirect(key_lists[0][:]))
+        nc.vector.tensor_copy(ks[0][:], key_scales[:].indirect(key_lists[0][:]))
+        nc.vector.tensor_copy(kw[1][:], key_words[:].indirect(key_lists[1][:]))
+        nc.vector.quantize_mx(out=q_codes[:].bitcast(FP8X4), scales=q_scales[:], in_=q_bf[:])
+        nc.vector.tensor_copy(ks[1][:], key_scales[:].indirect(key_lists[1][:]))
+
+        size_bank = ps.tile([P, PACK, P], F32, name="size_bank", tag="size")
+        for t in range(PACK):
+            nc.tensor.transpose(size_bank[:, t, :], size_cols[:, t : t + 1].to_broadcast([P, P]), ident[:])
+
+        score = [[None, None], [None, None]]
+        for s in range(2):
+            for h in range(HALVES):
+                score[h][s] = ps.tile([P, I], F32, name=f"score{h}{s}", tag=f"score{h}{s}")
+                nc.tensor.matmul_mx(
+                    out=score[h][s][:],
+                    lhsT=q_codes[:, h * P : (h + 1) * P].bitcast(FP8X4),
+                    lhsT_scale=q_scales[:, h * P : (h + 1) * P],
+                    rhs=kw[s][:].bitcast(FP4X4),
+                    rhs_scale=ks[s][:],
+                    start=True,
+                    stop=True,
+                )
+        neg_max = [sb.tile([P, 2], F32, name=f"neg_max{h}") for h in range(HALVES)]
+        shift = [sb.tile([P, 1], F32, name=f"shift{h}") for h in range(HALVES)]
+        for h in range(HALVES):
+            nc.vector.tensor_reduce(neg_max[h][:, 0:1], score[h][0][:], AX.X, ALU.max, negate=True)
+        nc.vector.tensor_reduce(neg_max[0][:, 1:2], score[0][1][:], AX.X, ALU.max, negate=True)
+        nc.vector.tensor_reduce(neg_max[1][:, 1:2], score[1][1][:], AX.X, ALU.max, negate=True)
+        for h in range(HALVES):
+            nc.vector.tensor_tensor(shift[h][:], neg_max[h][:, 0:1], neg_max[h][:, 1:2], ALU.min)
+        ex = [[sb.tile([P, I], F32, name=f"ex{h}{s}") for s in range(2)] for h in range(HALVES)]
+        for h in range(HALVES):
+            for s in range(2):
+                nc.scalar.activation(ex[h][s][:], score[h][s][:], ACT.Exp, bias=shift[h][:], scale=1.0)
+
+        v_codes = sb.tile([P, E], U32, name="v_codes", align_bytes=64)
+        v_scales = sb.tile([P, E], U8, name="v_scales", align_bytes=64)
+
+        def gather_vals(t):
+            picked = sb.tile([P, I], BF16, name=f"picked{t}", align_bytes=64)
+            nc.vector.tensor_copy(picked[:], val_pool[t][:].indirect(val_list[:]))
+            words = picked[:].bitcast(F32)
+            turned = ps.tile([P, 2, P], F32, name=f"turned{t}", tag=f"turned{t % 2}")
+            for u in range(2):
+                nc.tensor.transpose(turned[:, u, :], words[:, u : I // 2 : 2], ident[:])
+            v_bf = sb.tile([P, P * PACK], BF16, name=f"v_bf{t}", align_bytes=64)
+            nc.scalar.copy(v_bf[:].bitcast(F32).rearrange("p (c u) -> p c u", u=2), turned[:].rearrange("p u c -> p c u"))
+            return v_bf
+
+        def quantize_vals(t, v_bf):
+            cols = slice(t * P, (t + 1) * P)
+            nc.vector.quantize_mx(out=v_codes[:, cols].bitcast(FP8X4), scales=v_scales[:, cols], in_=v_bf[:])
+
+        v_bf0 = gather_vals(0)
+        v_bf1 = gather_vals(1)
+
+        w_bank = ps.tile([P, HALVES, 2, P], F32, name="w_bank", tag="w_bank")
+        w_bf = sb.tile([P, Q * PACK], BF16, name="w_bf", align_bytes=64)
+        pair = [sb.tile([P, I], F32, name=f"pair{h}") for h in range(HALVES)]
+        total = [sb.tile([P, 1], F32, name=f"total{h}") for h in range(HALVES)]
+        inverse = [sb.tile([P, 1], F32, name=f"inverse{h}") for h in range(HALVES)]
+        w_rows = [sb.tile([P, I], BF16, name=f"w_rows{h}") for h in range(HALVES)]
+        for h in range(HALVES):
+            nc.vector.scalar_tensor_tensor(pair[h][:], ex[h][0][:], 1.0, ex[h][1][:], ALU.mult, ALU.add, accum_out=total[h][:])
+        quantize_vals(0, v_bf0)
+        for h in range(HALVES):
+            nc.vector.reciprocal(inverse[h][:], total[h][:])
+        quantize_vals(1, v_bf1)
+        for h in range(HALVES):
+            nc.vector.scalar_tensor_tensor(
+                w_rows[h][:].rearrange("q (p t) -> q p t", t=PACK),
+                pair[h][:].rearrange("q (p t) -> q p t", t=PACK),
+                inverse[h][:],
+                size_bank[:].rearrange("q t p -> q p t"),
+                ALU.mult,
+                ALU.mult,
+            )
+            words = w_rows[h][:].bitcast(F32)
+            for u in range(2):
+                nc.tensor.transpose(w_bank[:, h, u, :], words[:, u : I // 2 : 2], ident[:])
+        nc.scalar.copy(
+            w_bf[:].bitcast(F32).rearrange("p (h c u) -> p h c u", h=HALVES, u=2),
+            w_bank[:].rearrange("p h u c -> p h c u"),
+        )
+        v_bf2 = gather_vals(2)
+        w_codes = sb.tile([P, Q], U32, name="w_codes", align_bytes=64)
+        w_scales = sb.tile([P, Q], U8, name="w_scales", align_bytes=64)
+        nc.vector.quantize_mx(out=w_codes[:].bitcast(FP8X4), scales=w_scales[:], in_=w_bf[:])
+        v_bf3 = gather_vals(3)
+        quantize_vals(2, v_bf2)
+        quantize_vals(3, v_bf3)
+
+        result = [ps.tile([P, PACK, P], F32, name=f"result{h}", tag=f"score{h}0") for h in range(HALVES)]
+        y = sb.tile([P, PACK, Q], F32, name="y")
+        y_rows = out_0.rearrange("(p t) q -> p t q", t=PACK)
+        for t in range(PACK):
+            for h in range(HALVES):
+                nc.tensor.matmul_mx(
+                    out=result[h][:, t, :],
+                    lhsT=v_codes[:, t * P : (t + 1) * P].bitcast(FP8X4),
+                    lhsT_scale=v_scales[:, t * P : (t + 1) * P],
+                    rhs=w_codes[:, h * P : (h + 1) * P].bitcast(FP8X4),
+                    rhs_scale=w_scales[:, h * P : (h + 1) * P],
+                    start=True,
+                    stop=True,
+                )
+            if t == 2:
+                for h in range(HALVES):
+                    nc.scalar.copy(y[:, 0:3, h * P : (h + 1) * P], result[h][:, 0:3, :])
+                nc.sync.dma_start(y_rows[:, 0:3, :], y[:, 0:3, :])
+        y_bf = sb.tile([P, Q * PACK], BF16, name="y_bf", align_bytes=64)
+        y_bf_view = y_bf[:].rearrange("p (h c t) -> p h c t", h=HALVES, t=PACK)
+        nc.vector.tensor_copy(y_bf_view[:, 0], result[0][:].rearrange("p t c -> p c t"))
+        nc.scalar.copy(y_bf_view[:, 1], result[1][:].rearrange("p t c -> p c t"))
+        for h in range(HALVES):
+            nc.scalar.copy(y[:, 3, h * P : (h + 1) * P], result[h][:, 3, :])
+        y_codes = sb.tile([P, Q], U32, name="y_codes", align_bytes=64)
+        y_scales = sb.tile([P, Q], U8, name="y_scales", align_bytes=64)
+        nc.vector.quantize_mx(out=y_codes[:].bitcast(FP8X4), scales=y_scales[:], in_=y_bf[:])
+        nc.sync.dma_start(out_1[0].rearrange("p c t -> p (c t)").bitcast(I32), y_codes[:].bitcast(I32))
+        for quad in range(4):
+            queue = nc.sync if quad < 2 else nc.scalar
+            queue.dma_start(
+                out_2[0, 4 * quad : 4 * quad + 4, :].bitcast(I32),
+                y_scales[32 * quad : 32 * quad + 4, :].bitcast(I32),
+            )
+        nc.scalar.dma_start(y_rows[:, 3, :], y[:, 3, :])

@@ -28,36 +28,42 @@ def tile_attend_synonyms_pl_kernel(tc, query, keys_words, keys_scales, size, val
     with ExitStack() as ctx:
         lists = ctx.enter_context(tc.tile_pool(name="lists", bufs=1))
         sb = ctx.enter_context(tc.tile_pool(name="sb", bufs=1))
+        late = ctx.enter_context(tc.tile_pool(name="late", bufs=1))
         ps = ctx.enter_context(tc.psum_pool(name="ps", bufs=1))
 
         key_scales = sb.tile([P, T], U8, name="key_scales", align_bytes=64)
-        nc.vector.memset(key_scales[:].bitcast(I32), 0)
+        nc.gpsimd.memset(key_scales[:].bitcast(I32), 0)
 
         key_lists = [lists.tile([P, I // 16], U16, name=f"key_list{s}") for s in range(2)]
         val_list = lists.tile([P, I // 16], U16, name="val_list")
         nc.sync.dma_start(key_lists[0][:], offs)
-        nc.sync.dma_start(key_lists[1][:], offs2)
         key_words = sb.tile([P, T], U16, name="key_words", align_bytes=64)
-        nc.sync.dma_start(key_words[:].bitcast(I32), keys_words[0].bitcast(I32))
+        nc.scalar.dma_start(key_words[:].bitcast(I32), keys_words[0].bitcast(I32))
+        nc.sync.dma_start(key_lists[1][:], offs2)
         for quad in range(4):
             nc.sync.dma_start(
                 key_scales[32 * quad : 32 * quad + 4, :].bitcast(I32),
                 keys_scales[0, 4 * quad : 4 * quad + 4, :].bitcast(I32),
             )
-        q_raw = sb.tile([P, PACK, Q], F32, name="q_raw")
+        q_raw = sb.tile([P, PACK, Q], F32, name="q_raw", tag="q_raw", align_bytes=64)
         nc.sync.dma_start(q_raw[:], query.rearrange("(p t) q -> p t q", t=PACK))
-        nc.sync.dma_start(val_list[:], offs3)
         val_rows = vals.rearrange("(p t) n -> t p n", t=PACK)
-        val_pool = [sb.tile([P, T], F32, name=f"val_pool{t}") for t in range(PACK)]
-        for t in range(PACK):
+        val_first = [sb.tile([P, T // 2], F32, name=f"val_first{j}") for j in range(2)]
+        for j in range(2):
+            nc.sync.dma_start(val_first[j][:], val_rows[0][:, j * (T // 2) : (j + 1) * (T // 2)])
+            if j == 0:
+                nc.sync.dma_start(val_list[:], offs3)
+        val_pool = [None] + [sb.tile([P, T], F32, name=f"val_pool{t}", tag=f"val_pool{t}", align_bytes=64) for t in range(1, PACK - 1)]
+        val_pool.append(late.tile([P, T], F32, name="val_pool3", offset=0, align_bytes=64))
+        for t in range(1, PACK):
             nc.sync.dma_start(val_pool[t][:], val_rows[t])
         size_cols = sb.tile([P, PACK], F32, name="size_cols")
-        nc.scalar.dma_start(size_cols[:], size[0].rearrange("(p t) -> p t", t=PACK))
+        nc.gpsimd.dma_start(size_cols[:], size[0].rearrange("(p t) -> p t", t=PACK))
 
         ident = sb.tile([P, P], F32, name="ident")
         make_identity(nc, ident[:])
 
-        q_bf = sb.tile([P, Q * PACK], BF16, name="q_bf", align_bytes=64)
+        q_bf = sb.tile([P, Q * PACK], BF16, name="q_bf", tag="q_bf", align_bytes=64)
         nc.scalar.copy(
             q_bf[:].rearrange("p (c i t) -> p c t i", i=4, t=PACK),
             q_raw[:].rearrange("p t (c i) -> p c t i", i=4),
@@ -66,23 +72,58 @@ def tile_attend_synonyms_pl_kernel(tc, query, keys_words, keys_scales, size, val
         q_scales = sb.tile([P, Q], U8, name="q_scales", align_bytes=64)
 
         kw = [sb.tile([P, I], U16, name=f"kw{s}", align_bytes=64) for s in range(2)]
-        ks = [sb.tile([P, I], U8, name=f"ks{s}", align_bytes=64) for s in range(2)]
+        ks = [sb.tile([P, I], U8, name="ks0", align_bytes=64), None]
         nc.vector.tensor_copy(kw[0][:], key_words[:].indirect(key_lists[0][:]))
         nc.vector.tensor_copy(ks[0][:], key_scales[:].indirect(key_lists[0][:]))
         nc.vector.tensor_copy(kw[1][:], key_words[:].indirect(key_lists[1][:]))
         nc.vector.quantize_mx(out=q_codes[:].bitcast(FP8X4), scales=q_scales[:], in_=q_bf[:])
+        ks[1] = sb.tile([P, I], U8, name="ks1", tag="q_raw", align_bytes=64)
         nc.vector.tensor_copy(ks[1][:], key_scales[:].indirect(key_lists[1][:]))
 
-        size_bank = ps.tile([P, PACK, P], F32, name="size_bank", tag="size")
-        for t in range(PACK):
-            nc.tensor.transpose(size_bank[:, t, :], size_cols[:, t : t + 1].to_broadcast([P, P]), ident[:])
+        v_bf = [sb.tile([P, 2 * I], BF16, name=f"v_bf{g}", tag=f"v_bf{g}", align_bytes=64) for g in range(2)]
 
-        score = [[None, None], [None, None]]
-        for s in range(2):
-            for h in range(HALVES):
-                score[h][s] = ps.tile([P, I], F32, name=f"score{h}{s}", tag=f"score{h}{s}")
+        def gather_vals(t):
+            picked = sb.tile([P, I], BF16, name=f"picked{t}", tag=("picked0", "neg_max1", "picked2", "picked3")[t], align_bytes=64)
+            if t == 0:
+                first_bf = sb.tile([P, T], BF16, name="first_bf", align_bytes=64)
+                for j in range(2):
+                    nc.scalar.activation(first_bf[:, j * (T // 2) : (j + 1) * (T // 2)], val_first[j][:], ACT.Copy)
+                nc.scalar.activation(picked[:], first_bf[:].indirect(val_list[:]), ACT.Copy)
+            else:
+                nc.vector.tensor_copy(picked[:], val_pool[t][:].indirect(val_list[:]))
+            return picked
+
+        def turn_vals(t, picked):
+            words = picked[:].bitcast(F32)
+            turned = ps.tile([P, 2, P], F32, name=f"turned{t}", tag=f"turned{t % 2}")
+            for u in range(2):
+                nc.tensor.transpose(turned[:, u, :], words[:, u : I // 2 : 2], ident[:])
+            nc.scalar.copy(
+                v_bf[t // 2][:, (t % 2) * I : (t % 2 + 1) * I].bitcast(F32).rearrange("p (c u) -> p c u", u=2),
+                turned[:].rearrange("p u c -> p c u"),
+            )
+
+        def quantize_vals(g):
+            if g == 0:
+                codes = late.tile([P, 2 * P], U32, name="v_codes0", offset=0, align_bytes=64)
+            else:
+                codes = sb.tile([P, 2 * P], U32, name="v_codes1", align_bytes=64)
+            scales = sb.tile([P, 2 * P], U8, name=f"v_scales{g}", align_bytes=64)
+            nc.vector.quantize_mx(out=codes[:].bitcast(FP8X4), scales=scales[:], in_=v_bf[g][:])
+            return codes, scales
+
+        picked0 = gather_vals(0)
+
+        ex = [[sb.tile([P, PACK, P], F32, name=f"ex{h}{s}") for s in range(2)] for h in range(HALVES)]
+        total = sb.tile([P, HALVES], F32, name="total")
+        sums = sb.tile([P, 2, HALVES], F32, name="sums")
+        for h in range(HALVES):
+            score = [ps.tile([P, I], F32, name=f"score{h}{s}", tag=f"score{h}{s}") for s in range(2)]
+            neg_max = sb.tile([P, 2], F32, name=f"neg_max{h}", tag=f"neg_max{h}", align_bytes=64)
+            shift = sb.tile([P, 1], F32, name=f"shift{h}")
+            for s in range(2):
                 nc.tensor.matmul_mx(
-                    out=score[h][s][:],
+                    out=score[s][:],
                     lhsT=q_codes[:, h * P : (h + 1) * P].bitcast(FP8X4),
                     lhsT_scale=q_scales[:, h * P : (h + 1) * P],
                     rhs=kw[s][:].bitcast(FP4X4),
@@ -90,108 +131,88 @@ def tile_attend_synonyms_pl_kernel(tc, query, keys_words, keys_scales, size, val
                     start=True,
                     stop=True,
                 )
-        neg_max = [sb.tile([P, 2], F32, name=f"neg_max{h}") for h in range(HALVES)]
-        shift = [sb.tile([P, 1], F32, name=f"shift{h}") for h in range(HALVES)]
-        for h in range(HALVES):
-            nc.vector.tensor_reduce(neg_max[h][:, 0:1], score[h][0][:], AX.X, ALU.max, negate=True)
-        nc.vector.tensor_reduce(neg_max[0][:, 1:2], score[0][1][:], AX.X, ALU.max, negate=True)
-        nc.vector.tensor_reduce(neg_max[1][:, 1:2], score[1][1][:], AX.X, ALU.max, negate=True)
-        for h in range(HALVES):
-            nc.vector.tensor_tensor(shift[h][:], neg_max[h][:, 0:1], neg_max[h][:, 1:2], ALU.min)
-        ex = [[sb.tile([P, I], F32, name=f"ex{h}{s}") for s in range(2)] for h in range(HALVES)]
-        for h in range(HALVES):
+                nc.vector.tensor_reduce(neg_max[:, s : s + 1], score[s][:], AX.X, ALU.max, negate=True)
+            nc.vector.tensor_tensor(shift[:], neg_max[:, 0:1], neg_max[:, 1:2], ALU.min)
             for s in range(2):
-                nc.scalar.activation(ex[h][s][:], score[h][s][:], ACT.Exp, bias=shift[h][:], scale=1.0)
+                nc.scalar.activation(
+                    ex[h][s][:], score[s][:].rearrange("q (p t) -> q t p", t=PACK), ACT.Exp,
+                    bias=shift[:], scale=1.0, accum_out=sums[:, s, h : h + 1],
+                )
+        nc.gpsimd.tensor_tensor(total[:], sums[:, 0, :], sums[:, 1, :], ALU.add)
 
-        v_codes = sb.tile([P, E], U32, name="v_codes", align_bytes=64)
-        v_scales = sb.tile([P, E], U8, name="v_scales", align_bytes=64)
+        def turn_weights(h):
+            bank = ps.tile([P, PACK, P], F32, name=f"p_bank{h}", tag=f"score{h}1")
+            for t in range(PACK):
+                for s in range(2):
+                    nc.tensor.matmul(bank[:, t, :], ex[h][s][:, t, :], ident[:], start=(s == 0), stop=(s == 1), is_transpose=True)
+            sized = sb.tile([P, PACK, P], F32, name=f"sized{h}")
+            for t in range(PACK):
+                nc.scalar.activation(sized[:, t, :], bank[:, t, :], ACT.Copy, scale=size_cols[:, t : t + 1])
+            return sized
 
-        def gather_vals(t):
-            picked = sb.tile([P, I], BF16, name=f"picked{t}", align_bytes=64)
-            nc.vector.tensor_copy(picked[:], val_pool[t][:].indirect(val_list[:]))
-            words = picked[:].bitcast(F32)
-            turned = ps.tile([P, 2, P], F32, name=f"turned{t}", tag=f"turned{t % 2}")
-            for u in range(2):
-                nc.tensor.transpose(turned[:, u, :], words[:, u : I // 2 : 2], ident[:])
-            v_bf = sb.tile([P, P * PACK], BF16, name=f"v_bf{t}", align_bytes=64)
-            nc.scalar.copy(v_bf[:].bitcast(F32).rearrange("p (c u) -> p c u", u=2), turned[:].rearrange("p u c -> p c u"))
-            return v_bf
-
-        def quantize_vals(t, v_bf):
-            cols = slice(t * P, (t + 1) * P)
-            nc.vector.quantize_mx(out=v_codes[:, cols].bitcast(FP8X4), scales=v_scales[:, cols], in_=v_bf[:])
-
-        v_bf0 = gather_vals(0)
-        v_bf1 = gather_vals(1)
-
-        w_bank = ps.tile([P, HALVES, 2, P], F32, name="w_bank", tag="w_bank")
-        w_bf = sb.tile([P, Q * PACK], BF16, name="w_bf", align_bytes=64)
-        pair = [sb.tile([P, I], F32, name=f"pair{h}") for h in range(HALVES)]
-        total = [sb.tile([P, 1], F32, name=f"total{h}") for h in range(HALVES)]
-        inverse = [sb.tile([P, 1], F32, name=f"inverse{h}") for h in range(HALVES)]
-        w_rows = [sb.tile([P, I], BF16, name=f"w_rows{h}") for h in range(HALVES)]
+        sized = [turn_weights(0)]
+        turn_vals(0, picked0)
+        turn_vals(1, gather_vals(1))
+        sized.append(turn_weights(1))
+        picked2 = gather_vals(2)
+        inverse = sb.tile([P, HALVES], F32, name="inverse", tag="val_pool2", align_bytes=64)
+        nc.vector.reciprocal(inverse[:], total[:])
+        inverse_bank = ps.tile([P, HALVES, P], F32, name="inverse_bank", tag="inverse")
         for h in range(HALVES):
-            nc.vector.scalar_tensor_tensor(pair[h][:], ex[h][0][:], 1.0, ex[h][1][:], ALU.mult, ALU.add, accum_out=total[h][:])
-        quantize_vals(0, v_bf0)
-        for h in range(HALVES):
-            nc.vector.reciprocal(inverse[h][:], total[h][:])
-        quantize_vals(1, v_bf1)
-        for h in range(HALVES):
-            nc.vector.scalar_tensor_tensor(
-                w_rows[h][:].rearrange("q (p t) -> q p t", t=PACK),
-                pair[h][:].rearrange("q (p t) -> q p t", t=PACK),
-                inverse[h][:],
-                size_bank[:].rearrange("q t p -> q p t"),
-                ALU.mult,
+            nc.tensor.transpose(inverse_bank[:, h, :], inverse[:, h : h + 1].to_broadcast([P, P]), ident[:])
+        turn_vals(2, picked2)
+        turn_vals(3, gather_vals(3))
+
+        def finish_weights(h):
+            w_bf = late.tile([P, I], BF16, name=f"w_bf{h}", offset=1024 * (h + 1), align_bytes=64)
+            nc.vector.tensor_tensor(
+                w_bf[:].rearrange("p (c i t) -> p c t i", i=4, t=PACK),
+                sized[h][:].rearrange("p t (c i) -> p c t i", i=4),
+                inverse_bank[:, h, :].rearrange("p (c i) -> p c i", i=4).unsqueeze(2).to_broadcast([P, P // 4, PACK, 4]),
                 ALU.mult,
             )
-            words = w_rows[h][:].bitcast(F32)
-            for u in range(2):
-                nc.tensor.transpose(w_bank[:, h, u, :], words[:, u : I // 2 : 2], ident[:])
-        nc.scalar.copy(
-            w_bf[:].bitcast(F32).rearrange("p (h c u) -> p h c u", h=HALVES, u=2),
-            w_bank[:].rearrange("p h u c -> p h c u"),
-        )
-        v_bf2 = gather_vals(2)
-        w_codes = sb.tile([P, Q], U32, name="w_codes", align_bytes=64)
-        w_scales = sb.tile([P, Q], U8, name="w_scales", align_bytes=64)
-        nc.vector.quantize_mx(out=w_codes[:].bitcast(FP8X4), scales=w_scales[:], in_=w_bf[:])
-        v_bf3 = gather_vals(3)
-        quantize_vals(2, v_bf2)
-        quantize_vals(3, v_bf3)
+            v_mx.append(quantize_vals(h))
+            codes = sb.tile([P, P], U32, name=f"w_codes{h}", align_bytes=64)
+            scales = sb.tile([P, P], U8, name=f"w_scales{h}", align_bytes=64)
+            nc.vector.quantize_mx(out=codes[:].bitcast(FP8X4), scales=scales[:], in_=w_bf[:])
+            return codes, scales
 
-        result = [ps.tile([P, PACK, P], F32, name=f"result{h}", tag=f"score{h}0") for h in range(HALVES)]
-        y = sb.tile([P, PACK, Q], F32, name="y")
         y_rows = out_0.rearrange("(p t) q -> p t q", t=PACK)
-        for t in range(PACK):
-            for h in range(HALVES):
+        y_codes = sb.tile([P, Q], U32, name="y_codes", align_bytes=64)
+        y_scales = sb.tile([P, Q], U8, name="y_scales", align_bytes=64)
+
+        def multiply(h, g):
+            bank = ps.tile([P, 2, P], F32, name=f"result{h}{g}", tag=f"score{g}{h}")
+            for j in range(2):
                 nc.tensor.matmul_mx(
-                    out=result[h][:, t, :],
-                    lhsT=v_codes[:, t * P : (t + 1) * P].bitcast(FP8X4),
-                    lhsT_scale=v_scales[:, t * P : (t + 1) * P],
-                    rhs=w_codes[:, h * P : (h + 1) * P].bitcast(FP8X4),
-                    rhs_scale=w_scales[:, h * P : (h + 1) * P],
+                    out=bank[:, j, :],
+                    lhsT=v_mx[g][0][:, j * P : (j + 1) * P].bitcast(FP8X4),
+                    lhsT_scale=v_mx[g][1][:, j * P : (j + 1) * P],
+                    rhs=w_mx[h][0][:].bitcast(FP8X4),
+                    rhs_scale=w_mx[h][1][:],
                     start=True,
                     stop=True,
                 )
-            if t == 2:
-                for h in range(HALVES):
-                    nc.scalar.copy(y[:, 0:3, h * P : (h + 1) * P], result[h][:, 0:3, :])
-                nc.sync.dma_start(y_rows[:, 0:3, :], y[:, 0:3, :])
-        y_bf = sb.tile([P, Q * PACK], BF16, name="y_bf", align_bytes=64)
-        y_bf_view = y_bf[:].rearrange("p (h c t) -> p h c t", h=HALVES, t=PACK)
-        nc.vector.tensor_copy(y_bf_view[:, 0], result[0][:].rearrange("p t c -> p c t"))
-        nc.scalar.copy(y_bf_view[:, 1], result[1][:].rearrange("p t c -> p c t"))
+            nc.scalar.copy(y[h][:, 2 * g : 2 * g + 2, :], bank[:])
+
+        v_mx = []
+        w_mx = [finish_weights(h) for h in range(HALVES)]
+        y = [sb.tile([P, PACK, P], F32, name=f"y{h}") for h in range(HALVES)]
         for h in range(HALVES):
-            nc.scalar.copy(y[:, 3, h * P : (h + 1) * P], result[h][:, 3, :])
-        y_codes = sb.tile([P, Q], U32, name="y_codes", align_bytes=64)
-        y_scales = sb.tile([P, Q], U8, name="y_scales", align_bytes=64)
+            for g in range(2):
+                multiply(h, g)
+            nc.sync.dma_start(y_rows[:, :, h * P : (h + 1) * P], y[h][:])
+        y_bf = sb.tile([P, Q * PACK], BF16, name="y_bf", align_bytes=64)
+        for h in range(HALVES):
+            nc.vector.tensor_copy(
+                y_bf[:, h * I : (h + 1) * I].rearrange("p (c i t) -> p c t i", i=4, t=PACK),
+                y[h][:].rearrange("p t (c i) -> p c t i", i=4),
+            )
         nc.vector.quantize_mx(out=y_codes[:].bitcast(FP8X4), scales=y_scales[:], in_=y_bf[:])
         nc.sync.dma_start(out_1[0].rearrange("p c t -> p (c t)").bitcast(I32), y_codes[:].bitcast(I32))
         for quad in range(4):
-            queue = nc.sync if quad < 2 else nc.scalar
+            queue = nc.scalar if quad < 2 else nc.sync
             queue.dma_start(
                 out_2[0, 4 * quad : 4 * quad + 4, :].bitcast(I32),
                 y_scales[32 * quad : 32 * quad + 4, :].bitcast(I32),
             )
-        nc.scalar.dma_start(y_rows[:, 3, :], y[:, 3, :])

from contextlib import ExitStack

import concourse.mybir as mybir
from concourse.masks import make_identity

D, T, I, Q, E = 512, 2048, 512, 256, 512
FLOPS = 2 * (2 * D * Q * I + I * E * Q)

F32 = mybir.dt.float32
BF16 = mybir.dt.bfloat16
I32 = mybir.dt.int32
U32 = mybir.dt.uint32
U16 = mybir.dt.uint16
U8 = mybir.dt.uint8
FP8X4 = mybir.dt.float8_e4m3fn_x4
FP4X4 = mybir.dt.float4_e2m1fn_x4
ALU = mybir.AluOpType
ACT = mybir.ActivationFunctionType
AX = mybir.AxisListType

P = 128
PACK = 4
HALVES = Q // P


def tile_attend_synonyms_pl_kernel(tc, query, keys_words, keys_scales, size, vals, offs, offs2, offs3, out_0, out_1, out_2):
    nc = tc.nc
    with ExitStack() as ctx:
        lists = ctx.enter_context(tc.tile_pool(name="lists", bufs=1))
        sb = ctx.enter_context(tc.tile_pool(name="sb", bufs=1))
        late = ctx.enter_context(tc.tile_pool(name="late", bufs=1))
        ps = ctx.enter_context(tc.psum_pool(name="ps", bufs=1))

        key_scales = sb.tile([P, T], U8, name="key_scales", align_bytes=64)
        nc.gpsimd.memset(key_scales[:].bitcast(I32), 0)

        key_lists = [lists.tile([P, I // 16], U16, name=f"key_list{s}") for s in range(2)]
        val_list = lists.tile([P, I // 16], U16, name="val_list")
        nc.sync.dma_start(key_lists[0][:], offs)
        key_words = sb.tile([P, T], U16, name="key_words", align_bytes=64)
        nc.scalar.dma_start(key_words[:].bitcast(I32), keys_words[0].bitcast(I32))
        nc.sync.dma_start(key_lists[1][:], offs2)
        for quad in range(4):
            nc.sync.dma_start(
                key_scales[32 * quad : 32 * quad + 4, :].bitcast(I32),
                keys_scales[0, 4 * quad : 4 * quad + 4, :].bitcast(I32),
            )
        q_raw = sb.tile([P, PACK, Q], F32, name="q_raw", tag="q_raw", align_bytes=64)
        nc.sync.dma_start(q_raw[:], query.rearrange("(p t) q -> p t q", t=PACK))
        val_rows = vals.rearrange("(p t) n -> t p n", t=PACK)
        val_first = [sb.tile([P, T // 2], F32, name=f"val_first{j}") for j in range(2)]
        for j in range(2):
            nc.sync.dma_start(val_first[j][:], val_rows[0][:, j * (T // 2) : (j + 1) * (T // 2)])
            if j == 0:
                nc.sync.dma_start(val_list[:], offs3)
        val_pool = [None] + [sb.tile([P, T], F32, name=f"val_pool{t}", tag=f"val_pool{t}", align_bytes=64) for t in range(1, PACK - 1)]
        val_pool.append(late.tile([P, T], F32, name="val_pool3", offset=0, align_bytes=64))
        for t in range(1, PACK):
            nc.sync.dma_start(val_pool[t][:], val_rows[t])
        size_cols = sb.tile([P, PACK], F32, name="size_cols")
        nc.gpsimd.dma_start(size_cols[:], size[0].rearrange("(p t) -> p t", t=PACK))

        ident = sb.tile([P, P], F32, name="ident")
        make_identity(nc, ident[:])

        q_bf = sb.tile([P, Q * PACK], BF16, name="q_bf", tag="q_bf", align_bytes=64)
        nc.scalar.copy(
            q_bf[:].rearrange("p (c i t) -> p c t i", i=4, t=PACK),
            q_raw[:].rearrange("p t (c i) -> p c t i", i=4),
        )
        q_codes = sb.tile([P, Q], U32, name="q_codes", align_bytes=64)
        q_scales = sb.tile([P, Q], U8, name="q_scales", align_bytes=64)

        kw = [sb.tile([P, I], U16, name=f"kw{s}", align_bytes=64) for s in range(2)]
        ks = [sb.tile([P, I], U8, name="ks0", align_bytes=64), None]
        nc.vector.tensor_copy(kw[0][:], key_words[:].indirect(key_lists[0][:]))
        nc.vector.tensor_copy(ks[0][:], key_scales[:].indirect(key_lists[0][:]))
        nc.vector.tensor_copy(kw[1][:], key_words[:].indirect(key_lists[1][:]))
        nc.vector.quantize_mx(out=q_codes[:].bitcast(FP8X4), scales=q_scales[:], in_=q_bf[:])
        ks[1] = sb.tile([P, I], U8, name="ks1", tag="q_raw", align_bytes=64)
        nc.vector.tensor_copy(ks[1][:], key_scales[:].indirect(key_lists[1][:]))

        v_bf = [sb.tile([P, 2 * I], BF16, name=f"v_bf{g}", tag=f"v_bf{g}", align_bytes=64) for g in range(2)]

        def gather_vals(t):
            picked = sb.tile([P, I], BF16, name=f"picked{t}", tag=("picked0", "neg_max1", "picked2", "picked3")[t], align_bytes=64)
            if t == 0:
                first_bf = sb.tile([P, T], BF16, name="first_bf", align_bytes=64)
                for j in range(2):
                    nc.scalar.activation(first_bf[:, j * (T // 2) : (j + 1) * (T // 2)], val_first[j][:], ACT.Copy)
                nc.scalar.activation(picked[:], first_bf[:].indirect(val_list[:]), ACT.Copy)
            else:
                nc.vector.tensor_copy(picked[:], val_pool[t][:].indirect(val_list[:]))
            return picked

        def turn_vals(t, picked):
            words = picked[:].bitcast(F32)
            turned = ps.tile([P, 2, P], F32, name=f"turned{t}", tag=f"turned{t % 2}")
            for u in range(2):
                nc.tensor.transpose(turned[:, u, :], words[:, u : I // 2 : 2], ident[:])
            nc.scalar.copy(
                v_bf[t // 2][:, (t % 2) * I : (t % 2 + 1) * I].bitcast(F32).rearrange("p (c u) -> p c u", u=2),
                turned[:].rearrange("p u c -> p c u"),
            )

        def quantize_vals(g):
            if g == 0:
                codes = late.tile([P, 2 * P], U32, name="v_codes0", offset=0, align_bytes=64)
            else:
                codes = sb.tile([P, 2 * P], U32, name="v_codes1", align_bytes=64)
            scales = sb.tile([P, 2 * P], U8, name=f"v_scales{g}", align_bytes=64)
            nc.vector.quantize_mx(out=codes[:].bitcast(FP8X4), scales=scales[:], in_=v_bf[g][:])
            return codes, scales

        picked0 = gather_vals(0)

        ex = [[sb.tile([P, PACK, P], F32, name=f"ex{h}{s}") for s in range(2)] for h in range(HALVES)]
        total = sb.tile([P, HALVES], F32, name="total")
        sums = sb.tile([P, 2, HALVES], F32, name="sums")
        for h in range(HALVES):
            score = [ps.tile([P, I], F32, name=f"score{h}{s}", tag=f"score{h}{s}") for s in range(2)]
            neg_max = sb.tile([P, 2], F32, name=f"neg_max{h}", tag=f"neg_max{h}", align_bytes=64)
            shift = sb.tile([P, 1], F32, name=f"shift{h}")
            for s in range(2):
                nc.tensor.matmul_mx(
                    out=score[s][:],
                    lhsT=q_codes[:, h * P : (h + 1) * P].bitcast(FP8X4),
                    lhsT_scale=q_scales[:, h * P : (h + 1) * P],
                    rhs=kw[s][:].bitcast(FP4X4),
                    rhs_scale=ks[s][:],
                    start=True,
                    stop=True,
                )
                nc.vector.tensor_reduce(neg_max[:, s : s + 1], score[s][:], AX.X, ALU.max, negate=True)
            nc.vector.tensor_tensor(shift[:], neg_max[:, 0:1], neg_max[:, 1:2], ALU.min)
            for s in range(2):
                nc.scalar.activation(
                    ex[h][s][:], score[s][:].rearrange("q (p t) -> q t p", t=PACK), ACT.Exp,
                    bias=shift[:], scale=1.0, accum_out=sums[:, s, h : h + 1],
                )
        nc.gpsimd.tensor_tensor(total[:], sums[:, 0, :], sums[:, 1, :], ALU.add)

        def turn_weights(h):
            bank = ps.tile([P, PACK, P], F32, name=f"p_bank{h}", tag=f"score{h}1")
            for t in range(PACK):
                for s in range(2):
                    nc.tensor.matmul(bank[:, t, :], ex[h][s][:, t, :], ident[:], start=(s == 0), stop=(s == 1), is_transpose=True)
            sized = sb.tile([P, PACK, P], F32, name=f"sized{h}")
            for t in range(PACK):
                nc.scalar.activation(sized[:, t, :], bank[:, t, :], ACT.Copy, scale=size_cols[:, t : t + 1])
            return sized

        sized = [turn_weights(0)]
        turn_vals(0, picked0)
        turn_vals(1, gather_vals(1))
        sized.append(turn_weights(1))
        picked2 = gather_vals(2)
        inverse = sb.tile([P, HALVES], F32, name="inverse", tag="val_pool2", align_bytes=64)
        nc.vector.reciprocal(inverse[:], total[:])
        inverse_bank = ps.tile([P, HALVES, P], F32, name="inverse_bank", tag="inverse")
        for h in range(HALVES):
            nc.tensor.transpose(inverse_bank[:, h, :], inverse[:, h : h + 1].to_broadcast([P, P]), ident[:])
        turn_vals(2, picked2)
        turn_vals(3, gather_vals(3))

        def finish_weights(h):
            w_bf = late.tile([P, I], BF16, name=f"w_bf{h}", offset=1024 * (h + 1), align_bytes=64)
            nc.vector.tensor_tensor(
                w_bf[:].rearrange("p (c i t) -> p c t i", i=4, t=PACK),
                sized[h][:].rearrange("p t (c i) -> p c t i", i=4),
                inverse_bank[:, h, :].rearrange("p (c i) -> p c i", i=4).unsqueeze(2).to_broadcast([P, P // 4, PACK, 4]),
                ALU.mult,
            )
            v_mx.append(quantize_vals(h))
            codes = sb.tile([P, P], U32, name=f"w_codes{h}", align_bytes=64)
            scales = sb.tile([P, P], U8, name=f"w_scales{h}", align_bytes=64)
            nc.vector.quantize_mx(out=codes[:].bitcast(FP8X4), scales=scales[:], in_=w_bf[:])
            return codes, scales

        y_rows = out_0.rearrange("(p t) q -> p t q", t=PACK)
        y_codes = sb.tile([P, Q], U32, name="y_codes", align_bytes=64)
        y_scales = sb.tile([P, Q], U8, name="y_scales", align_bytes=64)

        def multiply(h, g):
            bank = ps.tile([P, 2, P], F32, name=f"result{h}{g}", tag=f"score{g}{h}")
            for j in range(2):
                nc.tensor.matmul_mx(
                    out=bank[:, j, :],
                    lhsT=v_mx[g][0][:, j * P : (j + 1) * P].bitcast(FP8X4),
                    lhsT_scale=v_mx[g][1][:, j * P : (j + 1) * P],
                    rhs=w_mx[h][0][:].bitcast(FP8X4),
                    rhs_scale=w_mx[h][1][:],
                    start=True,
                    stop=True,
                )
            nc.scalar.copy(y[h][:, 2 * g : 2 * g + 2, :], bank[:])

        v_mx = []
        w_mx = [finish_weights(h) for h in range(HALVES)]
        y = [sb.tile([P, PACK, P], F32, name=f"y{h}") for h in range(HALVES)]
        for h in range(HALVES):
            for g in range(2):
                multiply(h, g)
            nc.sync.dma_start(y_rows[:, :, h * P : (h + 1) * P], y[h][:])
        y_bf = sb.tile([P, Q * PACK], BF16, name="y_bf", align_bytes=64)
        for h in range(HALVES):
            nc.vector.tensor_copy(
                y_bf[:, h * I : (h + 1) * I].rearrange("p (c i t) -> p c t i", i=4, t=PACK),
                y[h][:].rearrange("p t (c i) -> p c t i", i=4),
            )
        nc.vector.quantize_mx(out=y_codes[:].bitcast(FP8X4), scales=y_scales[:], in_=y_bf[:])
        nc.sync.dma_start(out_1[0].rearrange("p c t -> p (c t)").bitcast(I32), y_codes[:].bitcast(I32))
        for quad in range(4):
            queue = nc.scalar if quad < 2 else nc.sync
            queue.dma_start(
                out_2[0, 4 * quad : 4 * quad + 4, :].bitcast(I32),
                y_scales[32 * quad : 32 * quad + 4, :].bitcast(I32),
            )
